import numpy as np
import ml_dtypes


def mxq(x, axis, fmt="e4m3"):
    dtype, down = {"e4m3": (ml_dtypes.float8_e4m3fn, 7), "e5m2": (ml_dtypes.float8_e5m2, 14)}[fmt]
    v = np.moveaxis(np.asarray(x, np.float32).astype(ml_dtypes.bfloat16).astype(np.float64), axis, -1)
    blocks = v.reshape(v.shape[:-1] + (-1, 32))
    amax = np.abs(blocks).max(-1, keepdims=True)
    byte = np.maximum(np.where(amax > 0, np.frexp(amax)[1] - 1 + 127, 0) - down, 1)
    scale = np.exp2(byte - 127.0)
    codes = (blocks / scale).astype(np.float32).astype(dtype).astype(np.float64)
    return np.moveaxis((codes * scale).reshape(v.shape), -1, axis)


WIDE = False


def mx_kscale(k):
    if not WIDE:
        return np.ones(k)
    levels = np.array([10, -10, 5, -5, 0])
    if k % 512:
        return np.exp2(np.random.permutation(np.resize(levels, k // 32))).repeat(32)
    a = np.empty((k // 512, 16))
    for p in range(k // 512):
        a[p, :8] = np.random.permutation(np.resize(levels, 8))
        for g in range(8):
            far = levels[np.abs(levels - a[p, g]) >= 10]
            a[p, g + 8] = far[np.random.randint(len(far))]
    return np.exp2(a.ravel()).repeat(32)


def f64(x):
    return np.asarray(x).astype(np.float64)


def striped(idx):
    return np.tile(np.asarray(idx).reshape(-1, 16).T, (8, 1)).astype(np.uint16)


def unstriped(offs):
    return offs[:16].T.reshape(-1).astype(np.int64)


E2M1 = np.array([0.0, 0.5, 1.0, 1.5, 2.0, 3.0, 4.0, 6.0, -0.0, -0.5, -1.0, -1.5, -2.0, -3.0, -4.0, -6.0])


def pack_weight(w, fmt):
    k, n = w.shape
    w = f64(np.asarray(w, np.float32).astype(ml_dtypes.bfloat16)).reshape(k // 32, 32, n)
    amax = np.abs(w).max(1)
    if fmt == "e4m3":
        byte = np.frexp(amax)[1] - 1 + 127 - 7
    else:
        mant, ex = np.frexp(amax / 6.0)
        byte = np.where(mant > 0.5, ex, ex - 1) + 127
    byte = np.clip(np.where(amax > 0, byte, 1), 1, 254)
    scaled = (w * np.exp2(127.0 - byte)[:, None, :]).reshape(k, n).astype(np.float32)
    by_word = np.ascontiguousarray(scaled.reshape(k // 512, 128, 4, n).transpose(0, 1, 3, 2))
    if fmt == "e4m3":
        words = by_word.astype(ml_dtypes.float8_e4m3fn).view(np.uint8)
    else:
        c = by_word.astype(ml_dtypes.float4_e2m1fn).view(np.uint8) & 0xF
        words = (c[..., 0::2] | (c[..., 1::2] << 4)).reshape(k // 512, 128, 2 * n)
    return np.ascontiguousarray(words), np.ascontiguousarray(byte.astype(np.uint8).reshape(k // 512, 16, n))


def unpack_weight(words, scales, fmt):
    g, _, n = scales.shape
    words = np.ascontiguousarray(words).reshape(g, 128, n, -1)
    if fmt == "e4m3":
        vals = words.view(ml_dtypes.float8_e4m3fn).astype(np.float64)
    else:
        nib = np.empty((g, 128, n, 4), np.uint8)
        nib[..., 0::2] = words & 0xF
        nib[..., 1::2] = words >> 4
        vals = E2M1[nib]
    vals = vals * np.repeat(np.exp2(scales.astype(np.float64) - 127.0), 8, axis=1)[..., None]
    return vals.transpose(0, 1, 3, 2).reshape(g * 512, n)


def sigmoid(v):
    return 1.0 / (1.0 + np.exp(-v))


def bf(x):
    return np.asarray(x, np.float32).astype(ml_dtypes.bfloat16)


def planes(Y):
    r, m = Y.shape
    b = f64(bf(Y)).reshape(r // 32, 32, m)
    amax = np.abs(b).max(1)
    byte = np.clip(np.where(amax > 0, np.frexp(amax)[1] - 1 + 127 - 7, 1), 1, 254)
    codes = (b * np.exp2(127.0 - byte)[:, None, :]).reshape(r, m).astype(np.float32).astype(ml_dtypes.float8_e4m3fn).view(np.uint8)
    words = codes.reshape(r // 512, 128, 4, m).transpose(0, 1, 3, 2)
    return np.ascontiguousarray(words), np.ascontiguousarray(byte.astype(np.uint8).reshape(r // 512, 16, m))


D, T, I, Q, E, G, U = 512, 2048, 1024, 256, 512, 128, 512


def setup_inputs():
    n = np.random.standard_normal
    idx = np.random.permutation(T)[:I]
    idx2 = np.random.randint(0, U, G)
    fd = mx_kscale(D)
    fi = mx_kscale(I)
    ti = np.ones(T)
    ti[idx] = fi
    keysp = pack_weight(n((D, T)) / fd[:, None], "e2m1")
    return {
        "query": (n((D, Q)) * 0.5 / np.sqrt(D) * fd[:, None]).astype(np.float32),
        "keys_words": keysp[0],
        "keys_scales": keysp[1],
        "kind": (0.4 * n((Q, U))).astype(np.float32),
        "size": (np.random.uniform(4.0, 16.0, (1, I)) * fi).astype(np.float32),
        "vals": (n((E, T)) / ti).astype(np.float32),
        "offs": striped(idx),
        "offs2": striped(idx2),
    }


def reference(query, keys_words, keys_scales, kind, size, vals, offs, offs2):
    idx = unstriped(offs)
    idx2 = unstriped(offs2)
    keysu = unpack_weight(keys_words, keys_scales, "e2m1")
    queryq = mxq(f64(query), 0, "e4m3")
    keysidxg = keysu[:, idx]
    a = queryq.T @ keysidxg
    s = a.reshape(Q, G, I // G).mean(axis=2) + f64(kind)[:, idx2]
    p = np.exp(s - np.max(s, axis=1, keepdims=True))
    r = p / np.sum(p, axis=1, keepdims=True)
    rr = np.repeat(r, I // G, axis=1)
    w = rr * sigmoid(a) * f64(size)
    wt = w.T
    vt = f64(vals)[:, idx].T
    vtq = mxq(vt, 0, "e4m3")
    wtq = mxq(wt, 0, "e4m3")
    o = vtq.T @ wtq
    words, scales = planes(o)
    return o, words, scales

@@ -1,0 +1,248 @@
+from contextlib import ExitStack
+
+import concourse.mybir as mybir
+from concourse.masks import make_identity
+
+D, T, I, Q, E, G, U = 512, 2048, 1024, 256, 512, 128, 512
+FLOPS = 2 * D * I * Q + 2 * I * E * Q
+
+F32 = mybir.dt.float32
+BF16 = mybir.dt.bfloat16
+I32 = mybir.dt.int32
+U32 = mybir.dt.uint32
+U16 = mybir.dt.uint16
+U8 = mybir.dt.uint8
+FP8X4 = mybir.dt.float8_e4m3fn_x4
+FP4X4 = mybir.dt.float4_e2m1fn_x4
+ACT = mybir.ActivationFunctionType
+ALU = mybir.AluOpType
+AX = mybir.AxisListType
+
+P = 128
+PACK = 4
+KP = P * PACK
+SPAN = I // G
+PASSES = I // KP
+QB = Q // P
+SPANS_PER_PASS = KP // SPAN
+LIST_COLS = KP // 16
+
+
+def tile_attend_spanread_pl_kernel(tc, query, keys_words, keys_scales, kind, size, vals, offs, offs2, out_0, out_1, out_2):
+    nc = tc.nc
+    with ExitStack() as ctx:
+        sb = ctx.enter_context(tc.tile_pool(name="sb", bufs=1))
+        ps = ctx.enter_context(tc.psum_pool(name="ps", bufs=1))
+
+        def tile(name, shape, dtype):
+            return sb.tile(shape, dtype, name=name, align_bytes=64)
+
+        def bank(b):
+            return ps.tile([P, 512], F32, name="bank", tag="bank%d" % b)
+
+        key_scales = tile("key_scales", [P, T], U8)
+        nc.gpsimd.memset(key_scales[:].bitcast(I32), 0)
+        key_words = tile("key_words", [P, T], U16)
+        nc.sync.dma_start(key_words[:].bitcast(I32), keys_words[0].bitcast(I32))
+        slots = tile("slots", [P, I // 16], U16)
+        nc.sync.dma_start(slots[:], offs)
+        kinds = tile("kinds", [P, G // 16], U16)
+        nc.sync.dma_start(kinds[:], offs2)
+        size_col = tile("size_col", [P, PASSES, PACK], F32)
+        nc.sync.dma_start(size_col[:], size.rearrange("o (g p t) -> p (o g) t", p=P, t=PACK))
+        for quad in range(4):
+            nc.sync.dma_start(key_scales[32 * quad : 32 * quad + 4, :].bitcast(I32), keys_scales[0, 4 * quad : 4 * quad + 4, :].bitcast(I32))
+        q_raw = tile("q_raw", [P, PACK, Q], F32)
+        nc.sync.dma_start(q_raw[:], query.rearrange("(p j) q -> p j q", j=PACK))
+        val_rows = vals.rearrange("(p r) t -> r p t", r=PACK)
+        val_pool = [tile("val_pool%d" % r, [P, T], F32) for r in range(PACK)]
+        nc.sync.dma_start(val_pool[0][:], val_rows[0])
+        kind_pool = tile("kind_pool", [P, QB, U], F32)
+        nc.sync.dma_start(kind_pool[:], kind.rearrange("(b p) u -> p b u", p=P))
+        for r in range(1, PACK):
+            nc.sync.dma_start(val_pool[r][:], val_rows[r])
+
+        ident = tile("ident", [P, P], F32)
+        make_identity(nc, ident[:])
+        warm = tile("warm", [P, 1], F32)
+        nc.scalar.activation(warm[:], ident[:, 0:1], ACT.Sigmoid)
+
+        def pass_list(g):
+            return slots[:, g * LIST_COLS : (g + 1) * LIST_COLS]
+
+        q_bf = tile("q_bf", [P, Q, PACK], BF16)
+        nc.scalar.copy(q_bf[:], q_raw[:].rearrange("p j q -> p q j"))
+        q_codes = tile("q_codes", [P, Q], U32)
+        q_scales = tile("q_scales", [P, Q], U8)
+
+        scores = {}
+        for g in range(PASSES):
+            kw = tile("kw%d" % g, [P, KP], U16)
+            ksc = tile("ksc%d" % g, [P, KP], U8)
+            nc.vector.tensor_copy(kw[:], key_words[:].indirect(pass_list(g)))
+            nc.vector.tensor_copy(ksc[:], key_scales[:].indirect(pass_list(g)))
+            if g == 0:
+                nc.vector.quantize_mx(q_codes[:].bitcast(FP8X4), q_scales[:], q_bf[:].rearrange("p q j -> p (q j)"))
+            for b in range(QB):
+                cols = slice(b * P, (b + 1) * P)
+                scores[b, g] = bank(2 * g + b)
+                nc.tensor.matmul_mx(scores[b, g][:], q_codes[:, cols].bitcast(FP8X4), q_scales[:, cols], kw[:].bitcast(FP4X4), ksc[:], start=True, stop=True)
+
+        eighth = [tile("eighth%d" % b, [P, SPAN, G], F32) for b in range(QB)]
+        for g in range(PASSES):
+            for b in range(QB):
+                nc.scalar.activation(
+                    eighth[b][:, :, g * SPANS_PER_PASS : (g + 1) * SPANS_PER_PASS],
+                    scores[b, g][:].rearrange("q (s j) -> q j s", j=SPAN), ACT.Copy, scale=1.0 / SPAN)
+
+        gathered = {}
+
+        def gather_vals(r, g):
+            gathered[r, g] = tile("vg%d%d" % (r, g), [P, KP], BF16)
+            nc.vector.tensor_copy(gathered[r, g][:], val_pool[r][:].indirect(pass_list(g)))
+
+        v_codes = [tile("v_codes%d" % r, [P, PASSES * P], U32) for r in range(PACK)]
+        v_scales = [tile("v_scales%d" % r, [P, PASSES * P], U8) for r in range(PACK)]
+        v_bf = [tile("v_bf%d" % r, [P, PASSES * KP], BF16) for r in range(PACK)]
+
+        def turn_vals(r):
+            turned = bank(6 + r % 2)[:].rearrange("p (g u m) -> p g u m", g=PASSES, u=2)
+            for g in range(PASSES):
+                words = gathered[r, g][:].bitcast(F32)
+                for u in range(2):
+                    nc.tensor.transpose(turned[:, g, u, :], words[:, u : 2 * P : 2], ident[:])
+            nc.scalar.copy(v_bf[r][:].bitcast(F32).rearrange("p (g m u) -> p g m u", g=PASSES, u=2), turned.rearrange("p g u m -> p g m u"))
+
+        def quant_vals(r):
+            nc.vector.quantize_mx(v_codes[r][:].bitcast(FP8X4), v_scales[r][:], v_bf[r][:])
+
+        gather_vals(0, 0)
+        kind_g = tile("kind_g", [P, QB, G], F32)
+        for b in range(QB):
+            nc.vector.tensor_copy(kind_g[:, b, :], kind_pool[:, b, :].indirect(kinds[:]))
+        gather_vals(0, 1)
+
+        s_turned = bank(4)
+        for b in range(QB):
+            cols = slice(b * P, (b + 1) * P)
+            for j in range(SPAN):
+                nc.tensor.matmul(s_turned[:, cols], eighth[b][:, j, :], ident[:], start=(j == 0), stop=False, is_transpose=True)
+            nc.tensor.matmul(s_turned[:, cols], kind_g[:, b, :], ident[:], start=False, stop=True, is_transpose=True)
+
+        sig = {}
+        for g in range(PASSES):
+            for b in range(QB):
+                sig[b, g] = tile("sig%d%d" % (b, g), [P, PACK, P], F32)
+
+        def sigmoid(b, g):
+            nc.scalar.activation(sig[b, g][:], scores[b, g][:].rearrange("q (p t) -> q t p", t=PACK), ACT.Sigmoid)
+
+        sigmoid(0, 0)
+        sigmoid(1, 0)
+        s_sb = tile("s_sb", [P, Q], F32)
+        nc.scalar.copy(s_sb[:], s_turned[:, 0:Q])
+        s_bank = bank(5)
+        s = s_bank[:, 0 : QB * G].rearrange("q (b g) -> q b g", b=QB)
+        for b in range(QB):
+            nc.tensor.transpose(s[:, b, :], s_sb[:, b * P : (b + 1) * P], ident[:])
+        sigmoid(0, 1)
+        sigmoid(1, 1)
+        gather_vals(1, 0)
+        neg_max = tile("neg_max", [P, QB], F32)
+        nc.vector.tensor_reduce(neg_max[:], s, AX.X, ALU.max, negate=True)
+        gather_vals(1, 1)
+        turn_vals(0)
+
+        p_span = tile("p_span", [P, QB, G], F32)
+        row_sum = tile("row_sum", [P, QB], F32)
+        for b in range(QB):
+            nc.scalar.activation(p_span[:, b, :], s[:, b, :], ACT.Exp, bias=neg_max[:, b : b + 1], accum_out=row_sum[:, b : b + 1])
+        gather_vals(2, 0)
+        inv_sum = tile("inv_sum", [P, QB], F32)
+        nc.vector.reciprocal(inv_sum[:], row_sum[:])
+        quant_vals(0)
+
+        sized = tile("sized", [P, PASSES, PACK, Q], F32)
+
+        def turn_sig(g):
+            for half in range(2):
+                turned = bank(2 * g + half)[:].rearrange("p (t q) -> p t q", t=2)
+                for t in range(2):
+                    for b in range(QB):
+                        nc.tensor.transpose(turned[:, t, b * P : (b + 1) * P], sig[b, g][:, 2 * half + t, :], ident[:])
+                for t in range(2):
+                    nc.scalar.activation(sized[:, g, 2 * half + t, :], turned[:, t, :], ACT.Copy, scale=size_col[:, g, 2 * half + t : 2 * half + t + 1])
+
+        turn_sig(0)
+        r_twice = tile("r_twice", [P, QB, G, 2], F32)
+        for b in range(QB):
+            nc.scalar.activation(r_twice[:, b], p_span[:, b, :].unsqueeze(2).to_broadcast([P, G, 2]), ACT.Copy, scale=inv_sum[:, b : b + 1])
+        turn_vals(1)
+        gather_vals(2, 1)
+        r_turned = bank(4)[:].rearrange("p (g q) -> p g q", g=PASSES)
+        for b in range(QB):
+            r_cols = r_twice[:, b].rearrange("q g h -> q (g h)")
+            for g in range(PASSES):
+                nc.tensor.transpose(r_turned[:, g, b * P : (b + 1) * P], r_cols[:, g * P : (g + 1) * P], ident[:])
+        turn_sig(1)
+        gather_vals(3, 0)
+        quant_vals(1)
+        turn_vals(2)
+        gather_vals(3, 1)
+        turn_vals(3)
+
+        w_bf = [tile("w_bf%d" % b, [P, PASSES, P, PACK], BF16) for b in range(QB)]
+        w_codes = [tile("w_codes%d" % b, [P, PASSES * P], U32) for b in range(QB)]
+        w_scales = [tile("w_scales%d" % b, [P, PASSES * P], U8) for b in range(QB)]
+
+        def weights(b):
+            cols = slice(b * P, (b + 1) * P)
+            nc.vector.tensor_tensor(
+                w_bf[b][:], sized[:, :, :, cols].rearrange("p g t q -> p g q t"),
+                r_turned[:, :, cols].unsqueeze(3).to_broadcast([P, PASSES, P, PACK]), ALU.mult)
+
+        def quant_weights(b):
+            nc.vector.quantize_mx(w_codes[b][:].bitcast(FP8X4), w_scales[b][:], w_bf[b][:].rearrange("p g q t -> p (g q t)"))
+
+        o_codes = tile("o_codes", [P, Q], U32)
+        o_scales = tile("o_scales", [P, Q], U8)
+        out_rows = out_0.rearrange("(p r) q -> p r q", r=PACK)
+        out_words = out_1[0].rearrange("p c r -> p (c r)").bitcast(I32)
+        acc = {}
+        o_bf = {}
+
+        def product(b):
+            acc[b] = bank(5 if b == 0 else 0)[:].rearrange("p (r q) -> p r q", r=PACK)
+            for r in range(PACK):
+                for g in range(PASSES):
+                    k = slice(g * P, (g + 1) * P)
+                    nc.tensor.matmul_mx(acc[b][:, r, :], v_codes[r][:, k].bitcast(FP8X4), v_scales[r][:, k], w_codes[b][:, k].bitcast(FP8X4), w_scales[b][:, k], start=(g == 0), stop=(g == PASSES - 1))
+
+        def result(b):
+            cols = slice(b * P, (b + 1) * P)
+            o_f32 = tile("o_f32%d" % b, [P, PACK, P], F32)
+            nc.scalar.copy(o_f32[:], acc[b])
+            nc.sync.dma_start(out_rows[:, :, cols], o_f32[:])
+            o_bf[b] = tile("o_bf%d" % b, [P, P, PACK], BF16)
+            nc.vector.tensor_copy(o_bf[b][:], o_f32[:].rearrange("p r q -> p q r"))
+
+        def planes(b):
+            cols = slice(b * P, (b + 1) * P)
+            nc.vector.quantize_mx(o_codes[:, cols].bitcast(FP8X4), o_scales[:, cols], o_bf[b][:].rearrange("p q r -> p (q r)"))
+            nc.scalar.dma_start(out_words[:, cols], o_codes[:, cols].bitcast(I32))
+
+        weights(0)
+        quant_vals(2)
+        quant_weights(0)
+        quant_vals(3)
+        weights(1)
+        product(0)
+        quant_weights(1)
+        result(0)
+        product(1)
+        planes(0)
+        result(1)
+        planes(1)
+        for quad in range(4):
+            queue = nc.sync if quad % 2 == 0 else nc.scalar
+            queue.dma_start(out_2[0, 4 * quad : 4 * quad + 4, :].bitcast(I32), o_scales[32 * quad : 32 * quad + 4, :].bitcast(I32))

@@ -26,6 +26,7 @@ PASSES = I // KP
 QB = Q // P
 SPANS_PER_PASS = KP // SPAN
 LIST_COLS = KP // 16
+RUN = 4
 
 
 def tile_attend_spanread_pl_kernel(tc, query, keys_words, keys_scales, kind, size, vals, offs, offs2, out_0, out_1, out_2):
@@ -34,32 +35,36 @@ def tile_attend_spanread_pl_kernel(tc, query, keys_words, keys_scales, kind, siz
         sb = ctx.enter_context(tc.tile_pool(name="sb", bufs=1))
         ps = ctx.enter_context(tc.psum_pool(name="ps", bufs=1))
 
-        def tile(name, shape, dtype):
-            return sb.tile(shape, dtype, name=name, align_bytes=64)
+        def tile(name, shape, dtype, tag=None):
+            return sb.tile(shape, dtype, name=name, tag=tag or name, align_bytes=64)
 
         def bank(b):
             return ps.tile([P, 512], F32, name="bank", tag="bank%d" % b)
 
+        def q_cols(b):
+            return slice(b * P, (b + 1) * P)
+
         key_scales = tile("key_scales", [P, T], U8)
-        nc.gpsimd.memset(key_scales[:].bitcast(I32), 0)
+        nc.vector.memset(key_scales[:].bitcast(I32), 0)
         key_words = tile("key_words", [P, T], U16)
         nc.sync.dma_start(key_words[:].bitcast(I32), keys_words[0].bitcast(I32))
         slots = tile("slots", [P, I // 16], U16)
         nc.sync.dma_start(slots[:], offs)
-        kinds = tile("kinds", [P, G // 16], U16)
-        nc.sync.dma_start(kinds[:], offs2)
-        size_col = tile("size_col", [P, PASSES, PACK], F32)
-        nc.sync.dma_start(size_col[:], size.rearrange("o (g p t) -> p (o g) t", p=P, t=PACK))
-        for quad in range(4):
-            nc.sync.dma_start(key_scales[32 * quad : 32 * quad + 4, :].bitcast(I32), keys_scales[0, 4 * quad : 4 * quad + 4, :].bitcast(I32))
         q_raw = tile("q_raw", [P, PACK, Q], F32)
         nc.sync.dma_start(q_raw[:], query.rearrange("(p j) q -> p j q", j=PACK))
+        for quad in range(4):
+            nc.sync.dma_start(key_scales[32 * quad : 32 * quad + 4, :].bitcast(I32), keys_scales[0, 4 * quad : 4 * quad + 4, :].bitcast(I32))
         val_rows = vals.rearrange("(p r) t -> r p t", r=PACK)
         val_pool = [tile("val_pool%d" % r, [P, T], F32) for r in range(PACK)]
         nc.sync.dma_start(val_pool[0][:], val_rows[0])
         kind_pool = tile("kind_pool", [P, QB, U], F32)
         nc.sync.dma_start(kind_pool[:], kind.rearrange("(b p) u -> p b u", p=P))
-        for r in range(1, PACK):
+        kinds = tile("kinds", [P, G // 16], U16)
+        nc.sync.dma_start(kinds[:], offs2)
+        nc.sync.dma_start(val_pool[1][:], val_rows[1])
+        size_col = tile("size_col", [P, PASSES, PACK], F32)
+        nc.sync.dma_start(size_col[:], size.rearrange("o (g p t) -> p (o g) t", p=P, t=PACK))
+        for r in range(2, PACK):
             nc.sync.dma_start(val_pool[r][:], val_rows[r])
 
         ident = tile("ident", [P, P], F32)
@@ -71,42 +76,62 @@ def tile_attend_spanread_pl_kernel(tc, query, keys_words, keys_scales, kind, siz
             return slots[:, g * LIST_COLS : (g + 1) * LIST_COLS]
 
         q_bf = tile("q_bf", [P, Q, PACK], BF16)
-        nc.scalar.copy(q_bf[:], q_raw[:].rearrange("p j q -> p q j"))
+        nc.scalar.copy(q_bf[:].rearrange("p (c i) j -> p c j i", i=RUN), q_raw[:].rearrange("p j (c i) -> p c j i", i=RUN))
         q_codes = tile("q_codes", [P, Q], U32)
         q_scales = tile("q_scales", [P, Q], U8)
 
         scores = {}
         for g in range(PASSES):
             kw = tile("kw%d" % g, [P, KP], U16)
-            ksc = tile("ksc%d" % g, [P, KP], U8)
+            ksc = tile("ksc%d" % g, [P, KP], U8, tag="q_bf" if g == 1 else None)
             nc.vector.tensor_copy(kw[:], key_words[:].indirect(pass_list(g)))
             nc.vector.tensor_copy(ksc[:], key_scales[:].indirect(pass_list(g)))
             if g == 0:
                 nc.vector.quantize_mx(q_codes[:].bitcast(FP8X4), q_scales[:], q_bf[:].rearrange("p q j -> p (q j)"))
             for b in range(QB):
-                cols = slice(b * P, (b + 1) * P)
                 scores[b, g] = bank(2 * g + b)
-                nc.tensor.matmul_mx(scores[b, g][:], q_codes[:, cols].bitcast(FP8X4), q_scales[:, cols], kw[:].bitcast(FP4X4), ksc[:], start=True, stop=True)
+                nc.tensor.matmul_mx(scores[b, g][:], q_codes[:, q_cols(b)].bitcast(FP8X4), q_scales[:, q_cols(b)], kw[:].bitcast(FP4X4), ksc[:], start=True, stop=True)
 
-        eighth = [tile("eighth%d" % b, [P, SPAN, G], F32) for b in range(QB)]
+        span_sum = tile("span_sum", [P, QB, G], F32)
+        sig = {}
         for g in range(PASSES):
             for b in range(QB):
-                nc.scalar.activation(
-                    eighth[b][:, :, g * SPANS_PER_PASS : (g + 1) * SPANS_PER_PASS],
-                    scores[b, g][:].rearrange("q (s j) -> q j s", j=SPAN), ACT.Copy, scale=1.0 / SPAN)
+                nc.vector.tensor_reduce(span_sum[:, b, g * SPANS_PER_PASS : (g + 1) * SPANS_PER_PASS], scores[b, g][:].rearrange("q (s j) -> q s j", j=SPAN), AX.X, ALU.add)
+                sig[b, g] = tile("sig%d%d" % (b, g), [P, PACK, P], F32)
+                nc.scalar.activation(sig[b, g][:], scores[b, g][:].rearrange("q (p t) -> q t p", t=PACK), ACT.Sigmoid)
+
+        kind_g = tile("kind_g", [P, QB, G], F32)
+        for b in range(QB):
+            nc.vector.tensor_copy(kind_g[:, b, :], kind_pool[:, b, :].indirect(kinds[:]))
+        s = tile("s", [P, QB, G], F32)
+        nc.vector.scalar_tensor_tensor(s[:], span_sum[:], 1.0 / SPAN, kind_g[:], ALU.mult, ALU.add)
+        neg_max = tile("neg_max", [P, QB], F32)
+        nc.vector.tensor_reduce(neg_max[:], s[:], AX.X, ALU.max, negate=True)
+
+        sized = tile("sized", [P, PASSES, PACK, Q], F32)
+
+        def turn_sig(g):
+            for half in range(2):
+                turned = bank(4 + 2 * g + half)[:].rearrange("p (t q) -> p t q", t=2)
+                for t in range(2):
+                    for b in range(QB):
+                        nc.tensor.transpose(turned[:, t, q_cols(b)], sig[b, g][:, 2 * half + t, :], ident[:])
+                for t in range(2):
+                    nc.scalar.activation(sized[:, g, 2 * half + t, :], turned[:, t, :], ACT.Copy, scale=size_col[:, g, 2 * half + t : 2 * half + t + 1])
 
         gathered = {}
 
-        def gather_vals(r, g):
-            gathered[r, g] = tile("vg%d%d" % (r, g), [P, KP], BF16)
-            nc.vector.tensor_copy(gathered[r, g][:], val_pool[r][:].indirect(pass_list(g)))
+        def gather_vals(r):
+            for g in range(PASSES):
+                gathered[r, g] = tile("vg%d%d" % (r, g), [P, KP], BF16)
+                nc.vector.tensor_copy(gathered[r, g][:], val_pool[r][:].indirect(pass_list(g)))
 
         v_codes = [tile("v_codes%d" % r, [P, PASSES * P], U32) for r in range(PACK)]
-        v_scales = [tile("v_scales%d" % r, [P, PASSES * P], U8) for r in range(PACK)]
+        v_scales = {}
         v_bf = [tile("v_bf%d" % r, [P, PASSES * KP], BF16) for r in range(PACK)]
 
         def turn_vals(r):
-            turned = bank(6 + r % 2)[:].rearrange("p (g u m) -> p g u m", g=PASSES, u=2)
+            turned = bank(r)[:].rearrange("p (g u m) -> p g u m", g=PASSES, u=2)
             for g in range(PASSES):
                 words = gathered[r, g][:].bitcast(F32)
                 for u in range(2):
@@ -114,134 +139,96 @@ def tile_attend_spanread_pl_kernel(tc, query, keys_words, keys_scales, kind, siz
             nc.scalar.copy(v_bf[r][:].bitcast(F32).rearrange("p (g m u) -> p g m u", g=PASSES, u=2), turned.rearrange("p g u m -> p g m u"))
 
         def quant_vals(r):
+            v_scales[r] = tile("v_scales%d" % r, [P, PASSES * P], U8, tag="vg%d0" % (r + 1) if r + 1 < PACK else None)
             nc.vector.quantize_mx(v_codes[r][:].bitcast(FP8X4), v_scales[r][:], v_bf[r][:])
 
-        gather_vals(0, 0)
-        kind_g = tile("kind_g", [P, QB, G], F32)
-        for b in range(QB):
-            nc.vector.tensor_copy(kind_g[:, b, :], kind_pool[:, b, :].indirect(kinds[:]))
-        gather_vals(0, 1)
-
-        s_turned = bank(4)
-        for b in range(QB):
-            cols = slice(b * P, (b + 1) * P)
-            for j in range(SPAN):
-                nc.tensor.matmul(s_turned[:, cols], eighth[b][:, j, :], ident[:], start=(j == 0), stop=False, is_transpose=True)
-            nc.tensor.matmul(s_turned[:, cols], kind_g[:, b, :], ident[:], start=False, stop=True, is_transpose=True)
-
-        sig = {}
-        for g in range(PASSES):
-            for b in range(QB):
-                sig[b, g] = tile("sig%d%d" % (b, g), [P, PACK, P], F32)
-
-        def sigmoid(b, g):
-            nc.scalar.activation(sig[b, g][:], scores[b, g][:].rearrange("q (p t) -> q t p", t=PACK), ACT.Sigmoid)
-
-        sigmoid(0, 0)
-        sigmoid(1, 0)
-        s_sb = tile("s_sb", [P, Q], F32)
-        nc.scalar.copy(s_sb[:], s_turned[:, 0:Q])
-        s_bank = bank(5)
-        s = s_bank[:, 0 : QB * G].rearrange("q (b g) -> q b g", b=QB)
-        for b in range(QB):
-            nc.tensor.transpose(s[:, b, :], s_sb[:, b * P : (b + 1) * P], ident[:])
-        sigmoid(0, 1)
-        sigmoid(1, 1)
-        gather_vals(1, 0)
-        neg_max = tile("neg_max", [P, QB], F32)
-        nc.vector.tensor_reduce(neg_max[:], s, AX.X, ALU.max, negate=True)
-        gather_vals(1, 1)
-        turn_vals(0)
-
+        turn_sig(0)
         p_span = tile("p_span", [P, QB, G], F32)
         row_sum = tile("row_sum", [P, QB], F32)
         for b in range(QB):
             nc.scalar.activation(p_span[:, b, :], s[:, b, :], ACT.Exp, bias=neg_max[:, b : b + 1], accum_out=row_sum[:, b : b + 1])
-        gather_vals(2, 0)
-        inv_sum = tile("inv_sum", [P, QB], F32)
-        nc.vector.reciprocal(inv_sum[:], row_sum[:])
-        quant_vals(0)
-
-        sized = tile("sized", [P, PASSES, PACK, Q], F32)
-
-        def turn_sig(g):
-            for half in range(2):
-                turned = bank(2 * g + half)[:].rearrange("p (t q) -> p t q", t=2)
-                for t in range(2):
-                    for b in range(QB):
-                        nc.tensor.transpose(turned[:, t, b * P : (b + 1) * P], sig[b, g][:, 2 * half + t, :], ident[:])
-                for t in range(2):
-                    nc.scalar.activation(sized[:, g, 2 * half + t, :], turned[:, t, :], ACT.Copy, scale=size_col[:, g, 2 * half + t : 2 * half + t + 1])
-
-        turn_sig(0)
-        r_twice = tile("r_twice", [P, QB, G, 2], F32)
-        for b in range(QB):
-            nc.scalar.activation(r_twice[:, b], p_span[:, b, :].unsqueeze(2).to_broadcast([P, G, 2]), ACT.Copy, scale=inv_sum[:, b : b + 1])
-        turn_vals(1)
-        gather_vals(2, 1)
-        r_turned = bank(4)[:].rearrange("p (g q) -> p g q", g=PASSES)
-        for b in range(QB):
-            r_cols = r_twice[:, b].rearrange("q g h -> q (g h)")
-            for g in range(PASSES):
-                nc.tensor.transpose(r_turned[:, g, b * P : (b + 1) * P], r_cols[:, g * P : (g + 1) * P], ident[:])
         turn_sig(1)
-        gather_vals(3, 0)
-        quant_vals(1)
-        turn_vals(2)
-        gather_vals(3, 1)
-        turn_vals(3)
 
-        w_bf = [tile("w_bf%d" % b, [P, PASSES, P, PACK], BF16) for b in range(QB)]
-        w_codes = [tile("w_codes%d" % b, [P, PASSES * P], U32) for b in range(QB)]
-        w_scales = [tile("w_scales%d" % b, [P, PASSES * P], U8) for b in range(QB)]
+        def span_weights():
+            inv_sum = tile("inv_sum", [P, QB], F32, tag="val_pool2")
+            nc.vector.reciprocal(inv_sum[:], row_sum[:])
+            r_twice = tile("r_twice", [P, QB, G, 2], F32)
+            for b in range(QB):
+                nc.scalar.activation(r_twice[:, b], p_span[:, b, :].unsqueeze(2).to_broadcast([P, G, 2]), ACT.Copy, scale=inv_sum[:, b : b + 1])
+            turned = bank(4)[:].rearrange("p (g q) -> p g q", g=PASSES)
+            for b in range(QB):
+                r_cols = r_twice[:, b].rearrange("q g h -> q (g h)")
+                for g in range(PASSES):
+                    nc.tensor.transpose(turned[:, g, q_cols(b)], r_cols[:, g * P : (g + 1) * P], ident[:])
+            return turned
 
-        def weights(b):
-            cols = slice(b * P, (b + 1) * P)
+        for r in range(PACK):
+            gather_vals(r)
+            if r == 2:
+                r_turned = span_weights()
+            turn_vals(r)
+            if r > 0:
+                quant_vals(r - 1)
+
+        w_bf = tile("w_bf", [P, QB * PASSES * KP], BF16, tag="val_pool%d" % (PACK - 1))
+        w_codes = tile("w_codes", [P, QB * PASSES * P], U32)
+        w_scales = tile("w_scales", [P, QB * PASSES * P], U8)
+
+        def piece(b, g, width):
+            return slice((b * PASSES + g) * width, (b * PASSES + g + 1) * width)
+
+        def weights(b, g):
             nc.vector.tensor_tensor(
-                w_bf[b][:], sized[:, :, :, cols].rearrange("p g t q -> p g q t"),
-                r_turned[:, :, cols].unsqueeze(3).to_broadcast([P, PASSES, P, PACK]), ALU.mult)
+                w_bf[:, piece(b, g, KP)].rearrange("p (c i t) -> p c t i", i=RUN, t=PACK),
+                sized[:, g, :, q_cols(b)].rearrange("p t (c i) -> p c t i", i=RUN),
+                r_turned[:, g, q_cols(b)].rearrange("p (c i) -> p c i", i=RUN).unsqueeze(2).to_broadcast([P, P // RUN, PACK, RUN]),
+                ALU.mult)
 
-        def quant_weights(b):
-            nc.vector.quantize_mx(w_codes[b][:].bitcast(FP8X4), w_scales[b][:], w_bf[b][:].rearrange("p g q t -> p (g q t)"))
+        def quant_weights(b, g):
+            nc.vector.quantize_mx(w_codes[:, piece(b, g, P)].bitcast(FP8X4), w_scales[:, piece(b, g, P)], w_bf[:, piece(b, g, KP)])
+
+        def one_pass(acc, r, b, g):
+            k = slice(g * P, (g + 1) * P)
+            nc.tensor.matmul_mx(acc, v_codes[r][:, k].bitcast(FP8X4), v_scales[r][:, k], w_codes[:, piece(b, g, P)].bitcast(FP8X4), w_scales[:, piece(b, g, P)], start=(g == 0), stop=(g == PASSES - 1))
 
         o_codes = tile("o_codes", [P, Q], U32)
         o_scales = tile("o_scales", [P, Q], U8)
         out_rows = out_0.rearrange("(p r) q -> p r q", r=PACK)
         out_words = out_1[0].rearrange("p c r -> p (c r)").bitcast(I32)
-        acc = {}
-        o_bf = {}
-
-        def product(b):
-            acc[b] = bank(5 if b == 0 else 0)[:].rearrange("p (r q) -> p r q", r=PACK)
-            for r in range(PACK):
-                for g in range(PASSES):
-                    k = slice(g * P, (g + 1) * P)
-                    nc.tensor.matmul_mx(acc[b][:, r, :], v_codes[r][:, k].bitcast(FP8X4), v_scales[r][:, k], w_codes[b][:, k].bitcast(FP8X4), w_scales[b][:, k], start=(g == 0), stop=(g == PASSES - 1))
-
-        def result(b):
-            cols = slice(b * P, (b + 1) * P)
-            o_f32 = tile("o_f32%d" % b, [P, PACK, P], F32)
-            nc.scalar.copy(o_f32[:], acc[b])
-            nc.sync.dma_start(out_rows[:, :, cols], o_f32[:])
-            o_bf[b] = tile("o_bf%d" % b, [P, P, PACK], BF16)
-            nc.vector.tensor_copy(o_bf[b][:], o_f32[:].rearrange("p r q -> p q r"))
+        o_f32 = [tile("o_f32%d" % b, [P, PACK, P], F32) for b in range(QB)]
+        o_bf = [tile("o_bf%d" % b, [P, P, PACK], BF16) for b in range(QB)]
 
         def planes(b):
-            cols = slice(b * P, (b + 1) * P)
-            nc.vector.quantize_mx(o_codes[:, cols].bitcast(FP8X4), o_scales[:, cols], o_bf[b][:].rearrange("p q r -> p (q r)"))
-            nc.scalar.dma_start(out_words[:, cols], o_codes[:, cols].bitcast(I32))
+            nc.vector.quantize_mx(o_codes[:, q_cols(b)].bitcast(FP8X4), o_scales[:, q_cols(b)], o_bf[b][:].rearrange("p q r -> p (q r)"))
+            nc.scalar.dma_start(out_words[:, q_cols(b)], o_codes[:, q_cols(b)].bitcast(I32))
 
-        weights(0)
-        quant_vals(2)
-        quant_weights(0)
-        quant_vals(3)
-        weights(1)
-        product(0)
-        quant_weights(1)
-        result(0)
-        product(1)
+        weights(0, 0)
+        weights(0, 1)
+        quant_weights(0, 0)
+        quant_vals(PACK - 1)
+        quant_weights(0, 1)
+        weights(1, 0)
+        weights(1, 1)
+        quant_weights(1, 0)
+        quant_weights(1, 1)
+
+        acc0 = bank(5)[:].rearrange("p (r q) -> p r q", r=PACK)
+        for r in range(PACK):
+            for g in range(PASSES):
+                one_pass(acc0[:, r, :], r, 0, g)
+        nc.scalar.copy(o_f32[0][:], acc0)
+        nc.sync.dma_start(out_rows[:, :, q_cols(0)], o_f32[0][:])
+        nc.scalar.copy(o_bf[0][:], acc0.rearrange("p r q -> p q r"))
+
+        acc1 = [bank(r)[:, 0:P] for r in range(PACK)]
+        for g in range(PASSES):
+            for r in range(PACK):
+                one_pass(acc1[r], r, 1, g)
         planes(0)
-        result(1)
+        for r in range(PACK):
+            nc.scalar.copy(o_f32[1][:, r, :], acc1[r])
+        nc.sync.dma_start(out_rows[:, :, q_cols(1)], o_f32[1][:])
+        nc.vector.tensor_copy(o_bf[1][:].rearrange("p (c i) r -> p c r i", i=RUN), o_f32[1][:].rearrange("p r (c i) -> p c r i", i=RUN))
         planes(1)
         for quad in range(4):
             queue = nc.sync if quad % 2 == 0 else nc.scalar

@@ -27,6 +27,7 @@ QB = Q // P
 SPANS_PER_PASS = KP // SPAN
 LIST_COLS = KP // 16
 RUN = 4
+SIG_BANKS = ((4, 5), (6, 4))
 
 
 def tile_attend_spanread_pl_kernel(tc, query, keys_words, keys_scales, kind, size, vals, offs, offs2, out_0, out_1, out_2):
@@ -57,13 +58,13 @@ def tile_attend_spanread_pl_kernel(tc, query, keys_words, keys_scales, kind, siz
         val_rows = vals.rearrange("(p r) t -> r p t", r=PACK)
         val_pool = [tile("val_pool%d" % r, [P, T], F32) for r in range(PACK)]
         nc.sync.dma_start(val_pool[0][:], val_rows[0])
+        size_col = tile("size_col", [P, PASSES, PACK], F32)
+        nc.sync.dma_start(size_col[:], size.rearrange("o (g p t) -> p (o g) t", p=P, t=PACK))
         kind_pool = tile("kind_pool", [P, QB, U], F32)
         nc.sync.dma_start(kind_pool[:], kind.rearrange("(b p) u -> p b u", p=P))
         kinds = tile("kinds", [P, G // 16], U16)
         nc.sync.dma_start(kinds[:], offs2)
         nc.sync.dma_start(val_pool[1][:], val_rows[1])
-        size_col = tile("size_col", [P, PASSES, PACK], F32)
-        nc.sync.dma_start(size_col[:], size.rearrange("o (g p t) -> p (o g) t", p=P, t=PACK))
         for r in range(2, PACK):
             nc.sync.dma_start(val_pool[r][:], val_rows[r])
 
@@ -92,27 +93,40 @@ def tile_attend_spanread_pl_kernel(tc, query, keys_words, keys_scales, kind, siz
                 scores[b, g] = bank(2 * g + b)
                 nc.tensor.matmul_mx(scores[b, g][:], q_codes[:, q_cols(b)].bitcast(FP8X4), q_scales[:, q_cols(b)], kw[:].bitcast(FP4X4), ksc[:], start=True, stop=True)
 
-        span_sum = tile("span_sum", [P, QB, G], F32)
+        span_sum = tile("span_sum", [P, G], F32)
+        eighth = tile("eighth", [P, SPAN, G], F32)
         sig = {}
         for g in range(PASSES):
+            spans = slice(g * SPANS_PER_PASS, (g + 1) * SPANS_PER_PASS)
+            nc.scalar.activation(eighth[:, :, spans], scores[1, g][:].rearrange("q (s j) -> q j s", j=SPAN), ACT.Copy, scale=1.0 / SPAN)
             for b in range(QB):
-                nc.vector.tensor_reduce(span_sum[:, b, g * SPANS_PER_PASS : (g + 1) * SPANS_PER_PASS], scores[b, g][:].rearrange("q (s j) -> q s j", j=SPAN), AX.X, ALU.add)
                 sig[b, g] = tile("sig%d%d" % (b, g), [P, PACK, P], F32)
                 nc.scalar.activation(sig[b, g][:], scores[b, g][:].rearrange("q (p t) -> q t p", t=PACK), ACT.Sigmoid)
+            nc.vector.tensor_reduce(span_sum[:, spans], scores[0, g][:].rearrange("q (s j) -> q s j", j=SPAN), AX.X, ALU.add)
 
         kind_g = tile("kind_g", [P, QB, G], F32)
-        for b in range(QB):
+        for b in (1, 0):
             nc.vector.tensor_copy(kind_g[:, b, :], kind_pool[:, b, :].indirect(kinds[:]))
-        s = tile("s", [P, QB, G], F32)
-        nc.vector.scalar_tensor_tensor(s[:], span_sum[:], 1.0 / SPAN, kind_g[:], ALU.mult, ALU.add)
-        neg_max = tile("neg_max", [P, QB], F32)
-        nc.vector.tensor_reduce(neg_max[:], s[:], AX.X, ALU.max, negate=True)
+        s_bank = bank(7)
+        for j in range(SPAN):
+            nc.tensor.matmul(s_bank[:, 0:P], eighth[:, j, :], ident[:], start=(j == 0), stop=False, is_transpose=True)
+        nc.tensor.matmul(s_bank[:, 0:P], kind_g[:, 1, :], ident[:], start=False, stop=True, is_transpose=True)
+        s_turned = tile("s_turned", [P, P], F32)
+        nc.scalar.copy(s_turned[:], s_bank[:, 0:P])
+        nc.tensor.transpose(s_bank[:, P : P + G], s_turned[:], ident[:])
+        first = tile("s_first", [P, G + SPAN], F32, tag="val_pool1")
+        nc.vector.scalar_tensor_tensor(first[:, 0:G], span_sum[:], 1.0 / SPAN, kind_g[:, 0, :], ALU.mult, ALU.add)
+        s = [first[:, 0:G], s_bank[:, P : P + G]]
+        max_first = tile("neg_max0", [P, 1], F32)
+        neg_max = [max_first[:], first[:, G : G + 1]]
+        for b in (1, 0):
+            nc.vector.tensor_reduce(neg_max[b], s[b], AX.X, ALU.max, negate=True)
 
         sized = tile("sized", [P, PASSES, PACK, Q], F32)
 
         def turn_sig(g):
             for half in range(2):
-                turned = bank(4 + 2 * g + half)[:].rearrange("p (t q) -> p t q", t=2)
+                turned = bank(SIG_BANKS[g][half])[:].rearrange("p (t q) -> p t q", t=2)
                 for t in range(2):
                     for b in range(QB):
                         nc.tensor.transpose(turned[:, t, q_cols(b)], sig[b, g][:, 2 * half + t, :], ident[:])
@@ -120,34 +134,42 @@ def tile_attend_spanread_pl_kernel(tc, query, keys_words, keys_scales, kind, siz
                     nc.scalar.activation(sized[:, g, 2 * half + t, :], turned[:, t, :], ACT.Copy, scale=size_col[:, g, 2 * half + t : 2 * half + t + 1])
 
         gathered = {}
+        LAST = PACK - 1
 
         def gather_vals(r):
-            for g in range(PASSES):
-                gathered[r, g] = tile("vg%d%d" % (r, g), [P, KP], BF16)
-                nc.vector.tensor_copy(gathered[r, g][:], val_pool[r][:].indirect(pass_list(g)))
+            if r < LAST:
+                whole = tile("gathered%d" % r, [P, I], BF16, tag={2: "s_turned"}.get(r))
+                nc.vector.tensor_copy(whole[:], val_pool[r][:].indirect(slots[:]))
+                for g in range(PASSES):
+                    gathered[r, g] = whole[:, g * KP : (g + 1) * KP]
+            else:
+                for g in range(PASSES):
+                    half = tile("gathered_last%d" % g, [P, KP], BF16, tag="neg_max0" if g == 0 else None)
+                    nc.vector.tensor_copy(half[:], val_pool[r][:].indirect(pass_list(g)))
+                    gathered[r, g] = half[:]
 
         v_codes = [tile("v_codes%d" % r, [P, PASSES * P], U32) for r in range(PACK)]
         v_scales = {}
-        v_bf = [tile("v_bf%d" % r, [P, PASSES * KP], BF16) for r in range(PACK)]
+        v_bf = {}
 
         def turn_vals(r):
-            turned = bank(r)[:].rearrange("p (g u m) -> p g u m", g=PASSES, u=2)
+            v_bf[r] = tile("v_bf%d" % r, [P, PASSES * KP], BF16, tag=None)
+            turned = bank((3, 7, 1, 2)[r])[:].rearrange("p (g u m) -> p g u m", g=PASSES, u=2)
             for g in range(PASSES):
-                words = gathered[r, g][:].bitcast(F32)
+                words = gathered[r, g].bitcast(F32)
                 for u in range(2):
                     nc.tensor.transpose(turned[:, g, u, :], words[:, u : 2 * P : 2], ident[:])
             nc.scalar.copy(v_bf[r][:].bitcast(F32).rearrange("p (g m u) -> p g m u", g=PASSES, u=2), turned.rearrange("p g u m -> p g m u"))
 
         def quant_vals(r):
-            v_scales[r] = tile("v_scales%d" % r, [P, PASSES * P], U8, tag="vg%d0" % (r + 1) if r + 1 < PACK else None)
-            nc.vector.quantize_mx(v_codes[r][:].bitcast(FP8X4), v_scales[r][:], v_bf[r][:])
+            nc.vector.quantize_mx(v_codes[r][:].bitcast(FP8X4), v_scales[r], v_bf[r][:])
 
         turn_sig(0)
-        p_span = tile("p_span", [P, QB, G], F32)
+        turn_sig(1)
+        p_span = tile("p_span", [P, QB, G], F32, tag="size_col")
         row_sum = tile("row_sum", [P, QB], F32)
         for b in range(QB):
-            nc.scalar.activation(p_span[:, b, :], s[:, b, :], ACT.Exp, bias=neg_max[:, b : b + 1], accum_out=row_sum[:, b : b + 1])
-        turn_sig(1)
+            nc.scalar.activation(p_span[:, b, :], s[b], ACT.Exp, bias=neg_max[b], accum_out=row_sum[:, b : b + 1])
 
         def span_weights():
             inv_sum = tile("inv_sum", [P, QB], F32, tag="val_pool2")
@@ -155,7 +177,7 @@ def tile_attend_spanread_pl_kernel(tc, query, keys_words, keys_scales, kind, siz
             r_twice = tile("r_twice", [P, QB, G, 2], F32)
             for b in range(QB):
                 nc.scalar.activation(r_twice[:, b], p_span[:, b, :].unsqueeze(2).to_broadcast([P, G, 2]), ACT.Copy, scale=inv_sum[:, b : b + 1])
-            turned = bank(4)[:].rearrange("p (g q) -> p g q", g=PASSES)
+            turned = bank(5)[:].rearrange("p (g q) -> p g q", g=PASSES)
             for b in range(QB):
                 r_cols = r_twice[:, b].rearrange("q g h -> q (g h)")
                 for g in range(PASSES):
@@ -167,10 +189,13 @@ def tile_attend_spanread_pl_kernel(tc, query, keys_words, keys_scales, kind, siz
             if r == 2:
                 r_turned = span_weights()
             turn_vals(r)
-            if r > 0:
-                quant_vals(r - 1)
+        all_scales = tile("v_scales", [P, PACK * PASSES * P], U8, tag="val_pool3")
+        for r in range(PACK):
+            v_scales[r] = all_scales[:, r * PASSES * P : (r + 1) * PASSES * P]
+        for r in range(LAST):
+            quant_vals(r)
 
-        w_bf = tile("w_bf", [P, QB * PASSES * KP], BF16, tag="val_pool%d" % (PACK - 1))
+        w_bf = tile("w_bf", [P, QB * PASSES * KP], BF16, tag="v_bf0")
         w_codes = tile("w_codes", [P, QB * PASSES * P], U32)
         w_scales = tile("w_scales", [P, QB * PASSES * P], U8)
 
@@ -199,8 +224,10 @@ def tile_attend_spanread_pl_kernel(tc, query, keys_words, keys_scales, kind, siz
         o_bf = [tile("o_bf%d" % b, [P, P, PACK], BF16) for b in range(QB)]
 
         def planes(b):
+            if b == 1:
+                nc.vector.tensor_copy(o_bf[b][:].rearrange("p (c i) r -> p c r i", i=RUN), o_f32[b][:].rearrange("p r (c i) -> p c r i", i=RUN))
             nc.vector.quantize_mx(o_codes[:, q_cols(b)].bitcast(FP8X4), o_scales[:, q_cols(b)], o_bf[b][:].rearrange("p q r -> p (q r)"))
-            nc.scalar.dma_start(out_words[:, q_cols(b)], o_codes[:, q_cols(b)].bitcast(I32))
+            nc.sync.dma_start(out_words[:, q_cols(b)], o_codes[:, q_cols(b)].bitcast(I32))
 
         weights(0, 0)
         weights(0, 1)
@@ -212,7 +239,7 @@ def tile_attend_spanread_pl_kernel(tc, query, keys_words, keys_scales, kind, siz
         quant_weights(1, 0)
         quant_weights(1, 1)
 
-        acc0 = bank(5)[:].rearrange("p (r q) -> p r q", r=PACK)
+        acc0 = bank(7)[:].rearrange("p (r q) -> p r q", r=PACK)
         for r in range(PACK):
             for g in range(PASSES):
                 one_pass(acc0[:, r, :], r, 0, g)
@@ -226,9 +253,8 @@ def tile_attend_spanread_pl_kernel(tc, query, keys_words, keys_scales, kind, siz
                 one_pass(acc1[r], r, 1, g)
         planes(0)
         for r in range(PACK):
-            nc.scalar.copy(o_f32[1][:, r, :], acc1[r])
+            (nc.scalar.copy if r % 2 == 0 else nc.vector.tensor_copy)(o_f32[1][:, r, :], acc1[r])
         nc.sync.dma_start(out_rows[:, :, q_cols(1)], o_f32[1][:])
-        nc.vector.tensor_copy(o_bf[1][:].rearrange("p (c i) r -> p c r i", i=RUN), o_f32[1][:].rearrange("p r (c i) -> p c r i", i=RUN))
         planes(1)
         for quad in range(4):
             queue = nc.sync if quad % 2 == 0 else nc.scalar

@@ -82,11 +82,13 @@ def tile_attend_spanread_pl_kernel(tc, query, keys_words, keys_scales, kind, siz
         q_scales = tile("q_scales", [P, Q], U8)
 
         scores = {}
+        keys_g = {}
         for g in range(PASSES):
             kw = tile("kw%d" % g, [P, KP], U16)
             ksc = tile("ksc%d" % g, [P, KP], U8, tag="q_bf" if g == 1 else None)
             nc.vector.tensor_copy(kw[:], key_words[:].indirect(pass_list(g)))
             nc.vector.tensor_copy(ksc[:], key_scales[:].indirect(pass_list(g)))
+            keys_g[g] = (kw, ksc)
             if g == 0:
                 nc.vector.quantize_mx(q_codes[:].bitcast(FP8X4), q_scales[:], q_bf[:].rearrange("p q j -> p (q j)"))
             for b in range(QB):
@@ -192,8 +194,6 @@ def tile_attend_spanread_pl_kernel(tc, query, keys_words, keys_scales, kind, siz
         all_scales = tile("v_scales", [P, PACK * PASSES * P], U8, tag="val_pool3")
         for r in range(PACK):
             v_scales[r] = all_scales[:, r * PASSES * P : (r + 1) * PASSES * P]
-        for r in range(LAST):
-            quant_vals(r)
 
         w_bf = tile("w_bf", [P, QB * PASSES * KP], BF16, tag="v_bf0")
         w_codes = tile("w_codes", [P, QB * PASSES * P], U32)
@@ -229,14 +229,19 @@ def tile_attend_spanread_pl_kernel(tc, query, keys_words, keys_scales, kind, siz
             nc.vector.quantize_mx(o_codes[:, q_cols(b)].bitcast(FP8X4), o_scales[:, q_cols(b)], o_bf[b][:].rearrange("p q r -> p (q r)"))
             nc.sync.dma_start(out_words[:, q_cols(b)], o_codes[:, q_cols(b)].bitcast(I32))
 
+        quant_vals(0)
+        quant_vals(1)
+        for b in (4, 6):
+            nc.tensor.matmul_mx(bank(b)[:], v_codes[1][:, 0:P].bitcast(FP8X4), v_scales[1][:, 0:P], keys_g[0][0][:].bitcast(FP4X4), keys_g[0][1][:], start=True, stop=True)
         weights(0, 0)
         weights(0, 1)
         quant_weights(0, 0)
-        quant_vals(PACK - 1)
+        quant_vals(2)
         quant_weights(0, 1)
         weights(1, 0)
-        weights(1, 1)
+        quant_vals(3)
         quant_weights(1, 0)
+        weights(1, 1)
         quant_weights(1, 1)
 
         acc0 = bank(7)[:].rearrange("p (r q) -> p r q", r=PACK)

from contextlib import ExitStack

import concourse.mybir as mybir
from concourse.masks import make_identity

D, T, I, Q, E, G, U = 512, 2048, 1024, 256, 512, 128, 512
FLOPS = 2 * D * I * Q + 2 * I * E * Q

F32 = mybir.dt.float32
BF16 = mybir.dt.bfloat16
I32 = mybir.dt.int32
U32 = mybir.dt.uint32
U16 = mybir.dt.uint16
U8 = mybir.dt.uint8
FP8X4 = mybir.dt.float8_e4m3fn_x4
FP4X4 = mybir.dt.float4_e2m1fn_x4
ACT = mybir.ActivationFunctionType
ALU = mybir.AluOpType
AX = mybir.AxisListType

P = 128
PACK = 4
KP = P * PACK
SPAN = I // G
PASSES = I // KP
QB = Q // P
SPANS_PER_PASS = KP // SPAN
LIST_COLS = KP // 16
RUN = 4
SIG_BANKS = ((4, 5), (6, 4))


def tile_attend_spanread_pl_kernel(tc, query, keys_words, keys_scales, kind, size, vals, offs, offs2, out_0, out_1, out_2):
    nc = tc.nc
    with ExitStack() as ctx:
        sb = ctx.enter_context(tc.tile_pool(name="sb", bufs=1))
        ps = ctx.enter_context(tc.psum_pool(name="ps", bufs=1))

        def tile(name, shape, dtype, tag=None):
            return sb.tile(shape, dtype, name=name, tag=tag or name, align_bytes=64)

        def bank(b):
            return ps.tile([P, 512], F32, name="bank", tag="bank%d" % b)

        def q_cols(b):
            return slice(b * P, (b + 1) * P)

        key_scales = tile("key_scales", [P, T], U8)
        nc.vector.memset(key_scales[:].bitcast(I32), 0)
        key_words = tile("key_words", [P, T], U16)
        nc.sync.dma_start(key_words[:].bitcast(I32), keys_words[0].bitcast(I32))
        slots = tile("slots", [P, I // 16], U16)
        nc.sync.dma_start(slots[:], offs)
        q_raw = tile("q_raw", [P, PACK, Q], F32)
        nc.sync.dma_start(q_raw[:], query.rearrange("(p j) q -> p j q", j=PACK))
        for quad in range(4):
            nc.sync.dma_start(key_scales[32 * quad : 32 * quad + 4, :].bitcast(I32), keys_scales[0, 4 * quad : 4 * quad + 4, :].bitcast(I32))
        val_rows = vals.rearrange("(p r) t -> r p t", r=PACK)
        val_pool = [tile("val_pool%d" % r, [P, T], F32) for r in range(PACK)]
        nc.sync.dma_start(val_pool[0][:], val_rows[0])
        size_col = tile("size_col", [P, PASSES, PACK], F32)
        nc.sync.dma_start(size_col[:], size.rearrange("o (g p t) -> p (o g) t", p=P, t=PACK))
        kind_pool = tile("kind_pool", [P, QB, U], F32)
        nc.sync.dma_start(kind_pool[:], kind.rearrange("(b p) u -> p b u", p=P))
        kinds = tile("kinds", [P, G // 16], U16)
        nc.sync.dma_start(kinds[:], offs2)
        nc.sync.dma_start(val_pool[1][:], val_rows[1])
        for r in range(2, PACK):
            nc.sync.dma_start(val_pool[r][:], val_rows[r])

        ident = tile("ident", [P, P], F32)
        make_identity(nc, ident[:])
        warm = tile("warm", [P, 1], F32)
        nc.scalar.activation(warm[:], ident[:, 0:1], ACT.Sigmoid)

        def pass_list(g):
            return slots[:, g * LIST_COLS : (g + 1) * LIST_COLS]

        q_bf = tile("q_bf", [P, Q, PACK], BF16)
        nc.scalar.copy(q_bf[:].rearrange("p (c i) j -> p c j i", i=RUN), q_raw[:].rearrange("p j (c i) -> p c j i", i=RUN))
        q_codes = tile("q_codes", [P, Q], U32)
        q_scales = tile("q_scales", [P, Q], U8)

        scores = {}
        keys_g = {}
        for g in range(PASSES):
            kw = tile("kw%d" % g, [P, KP], U16)
            ksc = tile("ksc%d" % g, [P, KP], U8, tag="q_bf" if g == 1 else None)
            nc.vector.tensor_copy(kw[:], key_words[:].indirect(pass_list(g)))
            nc.vector.tensor_copy(ksc[:], key_scales[:].indirect(pass_list(g)))
            keys_g[g] = (kw, ksc)
            if g == 0:
                nc.vector.quantize_mx(q_codes[:].bitcast(FP8X4), q_scales[:], q_bf[:].rearrange("p q j -> p (q j)"))
            for b in range(QB):
                scores[b, g] = bank(2 * g + b)
                nc.tensor.matmul_mx(scores[b, g][:], q_codes[:, q_cols(b)].bitcast(FP8X4), q_scales[:, q_cols(b)], kw[:].bitcast(FP4X4), ksc[:], start=True, stop=True)

        span_sum = tile("span_sum", [P, G], F32)
        eighth = tile("eighth", [P, SPAN, G], F32)
        sig = {}
        for g in range(PASSES):
            spans = slice(g * SPANS_PER_PASS, (g + 1) * SPANS_PER_PASS)
            nc.scalar.activation(eighth[:, :, spans], scores[1, g][:].rearrange("q (s j) -> q j s", j=SPAN), ACT.Copy, scale=1.0 / SPAN)
            for b in range(QB):
                sig[b, g] = tile("sig%d%d" % (b, g), [P, PACK, P], F32)
                nc.scalar.activation(sig[b, g][:], scores[b, g][:].rearrange("q (p t) -> q t p", t=PACK), ACT.Sigmoid)
            nc.vector.tensor_reduce(span_sum[:, spans], scores[0, g][:].rearrange("q (s j) -> q s j", j=SPAN), AX.X, ALU.add)

        kind_g = tile("kind_g", [P, QB, G], F32)
        for b in (1, 0):
            nc.vector.tensor_copy(kind_g[:, b, :], kind_pool[:, b, :].indirect(kinds[:]))
        s_bank = bank(7)
        for j in range(SPAN):
            nc.tensor.matmul(s_bank[:, 0:P], eighth[:, j, :], ident[:], start=(j == 0), stop=False, is_transpose=True)
        nc.tensor.matmul(s_bank[:, 0:P], kind_g[:, 1, :], ident[:], start=False, stop=True, is_transpose=True)
        s_turned = tile("s_turned", [P, P], F32)
        nc.scalar.copy(s_turned[:], s_bank[:, 0:P])
        nc.tensor.transpose(s_bank[:, P : P + G], s_turned[:], ident[:])
        first = tile("s_first", [P, G + SPAN], F32, tag="val_pool1")
        nc.vector.scalar_tensor_tensor(first[:, 0:G], span_sum[:], 1.0 / SPAN, kind_g[:, 0, :], ALU.mult, ALU.add)
        s = [first[:, 0:G], s_bank[:, P : P + G]]
        max_first = tile("neg_max0", [P, 1], F32)
        neg_max = [max_first[:], first[:, G : G + 1]]
        for b in (1, 0):
            nc.vector.tensor_reduce(neg_max[b], s[b], AX.X, ALU.max, negate=True)

        sized = tile("sized", [P, PASSES, PACK, Q], F32)

        def turn_sig(g):
            for half in range(2):
                turned = bank(SIG_BANKS[g][half])[:].rearrange("p (t q) -> p t q", t=2)
                for t in range(2):
                    for b in range(QB):
                        nc.tensor.transpose(turned[:, t, q_cols(b)], sig[b, g][:, 2 * half + t, :], ident[:])
                for t in range(2):
                    nc.scalar.activation(sized[:, g, 2 * half + t, :], turned[:, t, :], ACT.Copy, scale=size_col[:, g, 2 * half + t : 2 * half + t + 1])

        gathered = {}
        LAST = PACK - 1

        def gather_vals(r):
            if r < LAST:
                whole = tile("gathered%d" % r, [P, I], BF16, tag={2: "s_turned"}.get(r))
                nc.vector.tensor_copy(whole[:], val_pool[r][:].indirect(slots[:]))
                for g in range(PASSES):
                    gathered[r, g] = whole[:, g * KP : (g + 1) * KP]
            else:
                for g in range(PASSES):
                    half = tile("gathered_last%d" % g, [P, KP], BF16, tag="neg_max0" if g == 0 else None)
                    nc.vector.tensor_copy(half[:], val_pool[r][:].indirect(pass_list(g)))
                    gathered[r, g] = half[:]

        v_codes = [tile("v_codes%d" % r, [P, PASSES * P], U32) for r in range(PACK)]
        v_scales = {}
        v_bf = {}

        def turn_vals(r):
            v_bf[r] = tile("v_bf%d" % r, [P, PASSES * KP], BF16, tag=None)
            turned = bank((3, 7, 1, 2)[r])[:].rearrange("p (g u m) -> p g u m", g=PASSES, u=2)
            for g in range(PASSES):
                words = gathered[r, g].bitcast(F32)
                for u in range(2):
                    nc.tensor.transpose(turned[:, g, u, :], words[:, u : 2 * P : 2], ident[:])
            nc.scalar.copy(v_bf[r][:].bitcast(F32).rearrange("p (g m u) -> p g m u", g=PASSES, u=2), turned.rearrange("p g u m -> p g m u"))

        def quant_vals(r):
            nc.vector.quantize_mx(v_codes[r][:].bitcast(FP8X4), v_scales[r], v_bf[r][:])

        turn_sig(0)
        turn_sig(1)
        p_span = tile("p_span", [P, QB, G], F32, tag="size_col")
        row_sum = tile("row_sum", [P, QB], F32)
        for b in range(QB):
            nc.scalar.activation(p_span[:, b, :], s[b], ACT.Exp, bias=neg_max[b], accum_out=row_sum[:, b : b + 1])

        def span_weights():
            inv_sum = tile("inv_sum", [P, QB], F32, tag="val_pool2")
            nc.vector.reciprocal(inv_sum[:], row_sum[:])
            r_twice = tile("r_twice", [P, QB, G, 2], F32)
            for b in range(QB):
                nc.scalar.activation(r_twice[:, b], p_span[:, b, :].unsqueeze(2).to_broadcast([P, G, 2]), ACT.Copy, scale=inv_sum[:, b : b + 1])
            turned = bank(5)[:].rearrange("p (g q) -> p g q", g=PASSES)
            for b in range(QB):
                r_cols = r_twice[:, b].rearrange("q g h -> q (g h)")
                for g in range(PASSES):
                    nc.tensor.transpose(turned[:, g, q_cols(b)], r_cols[:, g * P : (g + 1) * P], ident[:])
            return turned

        for r in range(PACK):
            gather_vals(r)
            if r == 2:
                r_turned = span_weights()
            turn_vals(r)
        all_scales = tile("v_scales", [P, PACK * PASSES * P], U8, tag="val_pool3")
        for r in range(PACK):
            v_scales[r] = all_scales[:, r * PASSES * P : (r + 1) * PASSES * P]

        w_bf = tile("w_bf", [P, QB * PASSES * KP], BF16, tag="v_bf0")
        w_codes = tile("w_codes", [P, QB * PASSES * P], U32)
        w_scales = tile("w_scales", [P, QB * PASSES * P], U8)

        def piece(b, g, width):
            return slice((b * PASSES + g) * width, (b * PASSES + g + 1) * width)

        def weights(b, g):
            nc.vector.tensor_tensor(
                w_bf[:, piece(b, g, KP)].rearrange("p (c i t) -> p c t i", i=RUN, t=PACK),
                sized[:, g, :, q_cols(b)].rearrange("p t (c i) -> p c t i", i=RUN),
                r_turned[:, g, q_cols(b)].rearrange("p (c i) -> p c i", i=RUN).unsqueeze(2).to_broadcast([P, P // RUN, PACK, RUN]),
                ALU.mult)

        def quant_weights(b, g):
            nc.vector.quantize_mx(w_codes[:, piece(b, g, P)].bitcast(FP8X4), w_scales[:, piece(b, g, P)], w_bf[:, piece(b, g, KP)])

        def one_pass(acc, r, b, g):
            k = slice(g * P, (g + 1) * P)
            nc.tensor.matmul_mx(acc, v_codes[r][:, k].bitcast(FP8X4), v_scales[r][:, k], w_codes[:, piece(b, g, P)].bitcast(FP8X4), w_scales[:, piece(b, g, P)], start=(g == 0), stop=(g == PASSES - 1))

        o_codes = tile("o_codes", [P, Q], U32)
        o_scales = tile("o_scales", [P, Q], U8)
        out_rows = out_0.rearrange("(p r) q -> p r q", r=PACK)
        out_words = out_1[0].rearrange("p c r -> p (c r)").bitcast(I32)
        o_f32 = [tile("o_f32%d" % b, [P, PACK, P], F32) for b in range(QB)]
        o_bf = [tile("o_bf%d" % b, [P, P, PACK], BF16) for b in range(QB)]

        def planes(b):
            if b == 1:
                nc.vector.tensor_copy(o_bf[b][:].rearrange("p (c i) r -> p c r i", i=RUN), o_f32[b][:].rearrange("p r (c i) -> p c r i", i=RUN))
            nc.vector.quantize_mx(o_codes[:, q_cols(b)].bitcast(FP8X4), o_scales[:, q_cols(b)], o_bf[b][:].rearrange("p q r -> p (q r)"))
            nc.sync.dma_start(out_words[:, q_cols(b)], o_codes[:, q_cols(b)].bitcast(I32))

        quant_vals(0)
        quant_vals(1)
        for b in (4, 6):
            nc.tensor.matmul_mx(bank(b)[:], v_codes[1][:, 0:P].bitcast(FP8X4), v_scales[1][:, 0:P], keys_g[0][0][:].bitcast(FP4X4), keys_g[0][1][:], start=True, stop=True)
        weights(0, 0)
        weights(0, 1)
        quant_weights(0, 0)
        quant_vals(2)
        quant_weights(0, 1)
        weights(1, 0)
        quant_vals(3)
        quant_weights(1, 0)
        weights(1, 1)
        quant_weights(1, 1)

        acc0 = bank(7)[:].rearrange("p (r q) -> p r q", r=PACK)
        for r in range(PACK):
            for g in range(PASSES):
                one_pass(acc0[:, r, :], r, 0, g)
        nc.scalar.copy(o_f32[0][:], acc0)
        nc.sync.dma_start(out_rows[:, :, q_cols(0)], o_f32[0][:])
        nc.scalar.copy(o_bf[0][:], acc0.rearrange("p r q -> p q r"))

        acc1 = [bank(r)[:, 0:P] for r in range(PACK)]
        for g in range(PASSES):
            for r in range(PACK):
                one_pass(acc1[r], r, 1, g)
        planes(0)
        for r in range(PACK):
            (nc.scalar.copy if r % 2 == 0 else nc.vector.tensor_copy)(o_f32[1][:, r, :], acc1[r])
        nc.sync.dma_start(out_rows[:, :, q_cols(1)], o_f32[1][:])
        planes(1)
        for quad in range(4):
            queue = nc.sync if quad % 2 == 0 else nc.scalar
            queue.dma_start(out_2[0, 4 * quad : 4 * quad + 4, :].bitcast(I32), o_scales[32 * quad : 32 * quad + 4, :].bitcast(I32))
